import numpy as np
import ml_dtypes


def mxq(x, axis, fmt="e4m3"):
    dtype, down = {"e4m3": (ml_dtypes.float8_e4m3fn, 7), "e5m2": (ml_dtypes.float8_e5m2, 14)}[fmt]
    v = np.moveaxis(np.asarray(x, np.float32).astype(ml_dtypes.bfloat16).astype(np.float64), axis, -1)
    blocks = v.reshape(v.shape[:-1] + (-1, 32))
    amax = np.abs(blocks).max(-1, keepdims=True)
    byte = np.maximum(np.where(amax > 0, np.frexp(amax)[1] - 1 + 127, 0) - down, 1)
    scale = np.exp2(byte - 127.0)
    codes = (blocks / scale).astype(np.float32).astype(dtype).astype(np.float64)
    return np.moveaxis((codes * scale).reshape(v.shape), -1, axis)


WIDE = False


def mx_kscale(k):
    if not WIDE:
        return np.ones(k)
    levels = np.array([10, -10, 5, -5, 0])
    if k % 512:
        return np.exp2(np.random.permutation(np.resize(levels, k // 32))).repeat(32)
    a = np.empty((k // 512, 16))
    for p in range(k // 512):
        a[p, :8] = np.random.permutation(np.resize(levels, 8))
        for g in range(8):
            far = levels[np.abs(levels - a[p, g]) >= 10]
            a[p, g + 8] = far[np.random.randint(len(far))]
    return np.exp2(a.ravel()).repeat(32)


def f64(x):
    return np.asarray(x).astype(np.float64)


def striped(idx):
    return np.tile(idx.reshape(-1, 16).T, (8, 1)).astype(np.uint16)


def unstriped(offs):
    return offs[:16].T.reshape(-1).astype(np.int64)


def striped8(idx):
    return np.concatenate([x.reshape(-1, 16).T for x in idx]).astype(np.uint16)


def runs(offs, k):
    lists = np.stack([offs[16 * r : 16 * r + 16].T.reshape(-1) for r in range(8)]).astype(np.int64)
    return lists[np.arange(k) % 512 // 64]


def pack_weight(w):
    k, n = w.shape
    w = f64(np.asarray(w, np.float32).astype(ml_dtypes.bfloat16)).reshape(k // 32, 32, n)
    amax = np.abs(w).max(1)
    byte = np.clip(np.where(amax > 0, np.frexp(amax)[1] - 1 + 127 - 7, 1), 1, 254)
    scaled = (w * np.exp2(127.0 - byte)[:, None, :]).reshape(k, n).astype(np.float32)
    words = np.ascontiguousarray(scaled.reshape(k // 512, 128, 4, n).transpose(0, 1, 3, 2)).astype(ml_dtypes.float8_e4m3fn).view(np.uint8)
    return words, np.ascontiguousarray(byte.astype(np.uint8).reshape(k // 512, 16, n))


def unpack_weight(words, scales):
    g, p, n, _ = words.shape
    vals = np.ascontiguousarray(words).view(ml_dtypes.float8_e4m3fn).astype(np.float64) * np.repeat(np.exp2(scales.astype(np.float64) - 127.0), 8, axis=1)[..., None]
    return vals.transpose(0, 1, 3, 2).reshape(g * 512, n)


K, T, S, H, C = 512, 2048, 512, 512, 512


def setup_inputs():
    n = np.random.standard_normal
    s = mx_kscale(K)[:, None]
    packed_xT = pack_weight(n((K, T)) * s)
    return {
        "x_words": packed_xT[0],
        "x_scales": packed_xT[1],
        "w1": (n((K, H)) / np.sqrt(K) / s).astype(np.float32),
        "gs": (np.random.uniform(0.5, 1.5, (K, 1)) / s).astype(np.float32),
        "offs": striped(np.random.permutation(T)[:S]),
        "n1": striped8(np.stack([np.random.permutation(S) for _ in range(8)])),
        "cand": striped(np.random.permutation(T)[:C]),
        "n2": striped8(np.stack([np.random.permutation(S) for _ in range(8)])),
        "n3": striped8(np.stack([np.random.permutation(S) for _ in range(8)])),
    }


def reference(x_words, x_scales, w1, gs, offs, n1, cand, n2, n3):
    x_cand = unpack_weight(x_words, x_scales)[:, unstriped(cand)]
    xq = unpack_weight(x_words, x_scales)[:, unstriped(offs)]
    y = mxq(f64(w1), 0, "e4m3").T @ xq
    st = y - (y[np.arange(H)[:, None], runs(n1, H)])
    z = f64(gs) * (st - (0.5 * (st[np.arange(H)[:, None], runs(n1, H)])))
    s = 0.0625 * ((x_cand.T @ mxq(z, 0, "e4m3")))
    pa = s[np.arange(C)[:, None], runs(n2, C)]
    pb = s[np.arange(C)[:, None], runs(n3, C)]
    return np.maximum(np.minimum(s, pa), np.minimum(np.maximum(s, pa), pb))

@@ -1,0 +1,222 @@
+from contextlib import ExitStack
+
+import concourse.mybir as mybir
+
+K, T, S, H, C = 512, 2048, 512, 512, 512
+FLOPS = 2 * K * H * S + 2 * K * C * S
+
+F32 = mybir.dt.float32
+BF16 = mybir.dt.bfloat16
+I32 = mybir.dt.int32
+U32 = mybir.dt.uint32
+U16 = mybir.dt.uint16
+U8 = mybir.dt.uint8
+FP8X4 = mybir.dt.float8_e4m3fn_x4
+ALU = mybir.AluOpType
+COPY = mybir.ActivationFunctionType.Copy
+
+P = 128
+PACK = 4
+LIST_ROWS = 16
+HALF = S // 2
+Z_CHUNKS = ((0, 256), (256, 384), (384, 512))
+W_SPLIT = 64
+
+
+def tile_picked_candtwicemed_none_p_kernel(
+    tc, x_words, x_scales, w1, gs, offs, n1, cand, n2, n3, out
+):
+    nc = tc.nc
+    with ExitStack() as ctx:
+        keep = ctx.enter_context(tc.tile_pool(name="keep", bufs=1))
+        psum = ctx.enter_context(tc.psum_pool(name="psum", bufs=1))
+
+        def load_list(src, name):
+            tile = keep.tile([P, S // LIST_ROWS], U16, name=name)
+            nc.sync.dma_start(tile[:], src)
+            return tile
+
+        def entries(lst, lo, hi):
+            return lst[:, lo // LIST_ROWS : hi // LIST_ROWS]
+
+        scale_table = keep.tile([P, T], U8, name="scale_table", align_bytes=64)
+        offs_l = load_list(offs, "offs_l")
+        for q in range(4):
+            rows = x_scales[0, 4 * q : 4 * q + 4, :].bitcast(I32)
+            nc.sync.dma_start(
+                scale_table[32 * q : 32 * q + 32, :].bitcast(I32), rows.unsqueeze(0).to_broadcast([8, 4, T // 4])
+            )
+        cand_l = load_list(cand, "cand_l")
+        w_raw = keep.tile([P, PACK, H], F32, name="w_raw")
+        nc.sync.dma_start(w_raw[:], w1.rearrange("(p j) c -> p j c", j=PACK))
+        word_table = keep.tile([P, T], I32, name="word_table", align_bytes=64)
+        nc.sync.dma_start(word_table[:], x_words[0].rearrange("p n r -> p (n r)").bitcast(I32))
+        gain = keep.tile([P, PACK], F32, name="gain")
+        nc.sync.dma_start(gain[:], gs.rearrange("(p t) o -> p (t o)", t=PACK))
+        n1_l = load_list(n1, "n1_l")
+        n2_l = load_list(n2, "n2_l")
+        n3_l = load_list(n3, "n3_l")
+
+        xq_scales = keep.tile([P, S], U8, name="xq_scales", align_bytes=64)
+        nc.vector.tensor_copy(xq_scales[:], scale_table[:].indirect(offs_l[:]))
+        cand_scales_listed = keep.tile([P, C], U8, name="cand_scales_listed", align_bytes=64)
+        nc.vector.tensor_copy(cand_scales_listed[:], scale_table[:].indirect(cand_l[:]))
+
+        w_bf = keep.tile([P, PACK, P, PACK], BF16, name="w_bf", align_bytes=64)
+        w_dst = w_bf[:].rearrange("p t m j -> p m j t")
+        w_src = w_raw[:].rearrange("p j (m t) -> p m j t", t=PACK)
+        nc.scalar.copy(w_dst[:, W_SPLIT:P, :, 2:4], w_src[:, W_SPLIT:P, :, 2:4])
+        nc.vector.tensor_copy(w_dst[:, :, :, 0:2], w_src[:, :, :, 0:2])
+        nc.vector.tensor_copy(w_dst[:, 0:W_SPLIT, :, 2:4], w_src[:, 0:W_SPLIT, :, 2:4])
+        cand_scales = keep.tile([P, C], U8, name="cand_scales", align_bytes=64)
+        nc.vector.tensor_copy(
+            cand_scales[:].rearrange("p (t m) -> p m t", t=PACK),
+            cand_scales_listed[:].rearrange("p (m t) -> p m t", t=PACK),
+        )
+        w_codes = keep.tile([P, H], U32, name="w_codes", align_bytes=64)
+        w_scales = keep.tile([P, H], U8, name="w_scales", align_bytes=64)
+        for t in (0, 2):
+            cols = slice(t * P, (t + 2) * P)
+            nc.vector.quantize_mx(
+                out=w_codes[:, cols].bitcast(FP8X4),
+                scales=w_scales[:, cols],
+                in_=w_bf[:, t : t + 2].rearrange("p t m j -> p (t m j)"),
+            )
+
+        words = word_table[:].bitcast(U32)
+        xq_codes = keep.tile([P, S], U32, name="xq_codes", align_bytes=64)
+        for lo in (0, HALF):
+            nc.vector.tensor_copy(xq_codes[:, lo : lo + HALF], words.indirect(entries(offs_l, lo, lo + HALF)))
+        cand_codes = keep.tile([P, C], U32, name="cand_codes", align_bytes=64)
+        nc.vector.tensor_copy(cand_codes[:].rearrange("p (t m) -> p m t", t=PACK), words.indirect(cand_l[:]))
+
+        def product(bank, lhs_codes, lhs_scales, t, rhs_codes, rhs_scales, lo, hi):
+            acc = psum.tile([P, hi - lo], F32, name=f"acc{bank}", tag=f"bank{bank}")
+            rows = slice(t * P, (t + 1) * P)
+            nc.tensor.matmul_mx(
+                out=acc[:],
+                lhsT=lhs_codes[:, rows].bitcast(FP8X4),
+                lhsT_scale=lhs_scales[:, rows],
+                rhs=rhs_codes[:, lo:hi].bitcast(FP8X4),
+                rhs_scale=rhs_scales[:, lo:hi],
+                start=True,
+                stop=True,
+            )
+            return acc
+
+        def twin_tiles(name):
+            windows = [keep.tile([P, S if t == 0 else 2 * S], F32, name=f"{name}_win{t}") for t in range(PACK)]
+            last = keep.tile([P, S], F32, name=f"{name}_last")
+            plains = [windows[t + 1][:, S : 2 * S] for t in range(PACK - 1)] + [last[:]]
+            return windows, plains
+
+        def leave_psum(acc, window, plain, lo, hi, scale):
+            nc.scalar.activation(window[:, lo:hi], acc[:], COPY, scale=scale)
+            nc.scalar.activation(plain[:, lo:hi], acc[:], COPY, scale=scale)
+
+        def gather_minus(dst, window, lst, plain, lo, hi):
+            nc.vector.tensor_tensor(dst, window[:].indirect(entries(lst, lo, hi)), plain[:, lo:hi], ALU.subtract)
+
+        def spans(t):
+            return ((0, HALF), (HALF, S)) if t == 0 else ((0, S),)
+
+        y_win, y_plain = twin_tiles("y")
+        bank = 0
+        for t in range(PACK):
+            for lo, hi in spans(t):
+                acc = product(bank, w_codes, w_scales, t, xq_codes, xq_scales, lo, hi)
+                leave_psum(acc, y_win[t], y_plain[t], lo, hi, gain[:, t : t + 1])
+                bank = bank + 1
+
+        neg_st = [keep.tile([P, S], F32, name=f"neg_st{t}") for t in range(PACK)]
+        neg_half_st = [keep.tile([P, S], F32, name=f"neg_half_st{t}") for t in range(PACK)]
+        for t in range(PACK):
+            for lo, hi in spans(t):
+                gather_minus(neg_st[t][:, lo:hi], y_win[t], n1_l, y_plain[t], lo, hi)
+            nc.scalar.activation(neg_half_st[t][:], neg_st[t][:], COPY, scale=0.5)
+
+        z_codes = keep.tile([P, S], U32, name="z_codes", align_bytes=64)
+        z_scales = keep.tile([P, S], U8, name="z_scales", align_bytes=64)
+        s_win, s_plain = twin_tiles("s")
+        z_f32 = [keep.tile([P, PACK, hi - lo], F32, name=f"z_f32_{lo}") for lo, hi in Z_CHUNKS]
+        z_bf = [keep.tile([P, hi - lo, PACK], BF16, name=f"z_bf_{lo}", align_bytes=64) for lo, hi in Z_CHUNKS]
+
+        def z_gather(c):
+            lo, hi = Z_CHUNKS[c]
+            for t in range(PACK):
+                gather_minus(z_f32[c][:, t, :], neg_half_st[t], n1_l, neg_st[t], lo, hi)
+
+        def z_round(c, copy):
+            copy(
+                z_bf[c][:].rearrange("p (c i) t -> p c t i", i=4),
+                z_f32[c][:].rearrange("p t (c i) -> p c t i", i=4),
+            )
+
+        def z_quantize(c):
+            lo, hi = Z_CHUNKS[c]
+            nc.vector.quantize_mx(
+                out=z_codes[:, lo:hi].bitcast(FP8X4),
+                scales=z_scales[:, lo:hi],
+                in_=z_bf[c][:].rearrange("p n t -> p (n t)"),
+            )
+
+        def scores(bank, t, lo, hi):
+            acc = product(bank, cand_codes, cand_scales, t, z_codes, z_scales, lo, hi)
+            leave_psum(acc, s_win[t], s_plain[t], lo, hi, 0.0625)
+
+        z_gather(0)
+        z_round(0, nc.scalar.copy)
+        z_gather(1)
+        z_round(1, nc.scalar.copy)
+        z_quantize(0)
+        scores(5, 0, *Z_CHUNKS[0])
+        z_gather(2)
+        z_quantize(1)
+        scores(6, 0, *Z_CHUNKS[1])
+        scores(0, 1, *Z_CHUNKS[0])
+        scores(1, 1, *Z_CHUNKS[1])
+        z_round(2, nc.vector.tensor_copy)
+        z_quantize(2)
+        scores(7, 0, *Z_CHUNKS[2])
+        scores(2, 1, *Z_CHUNKS[2])
+        scores(3, 2, 0, S)
+        scores(4, 3, 0, S)
+
+        out_rows = out.rearrange("(p t) n -> p t n", t=PACK)
+        da = [keep.tile([P, S], F32, name=f"da{t}") for t in range(PACK)]
+        db = [keep.tile([P, S], F32, name=f"db{t}") for t in range(PACK)]
+        upper = [keep.tile([P, S], F32, name=f"upper{t}") for t in range(PACK)]
+        step = [keep.tile([P, S], F32, name=f"step{t}") for t in range(PACK)]
+        res = [keep.tile([P, S], F32, name=f"res{t}") for t in range(PACK)]
+
+        def fetch(dst, lst, t):
+            for lo, hi in spans(t):
+                gather_minus(dst[t][:, lo:hi], s_win[t], lst, s_plain[t], lo, hi)
+
+        def clip_above(t, lo=0, hi=S):
+            nc.vector.scalar_tensor_tensor(upper[t][:, lo:hi], da[t][:, lo:hi], 0.0, db[t][:, lo:hi], ALU.max, ALU.min)
+
+        def clip_below(t, lo=0, hi=S):
+            nc.vector.scalar_tensor_tensor(step[t][:, lo:hi], da[t][:, lo:hi], 0.0, upper[t][:, lo:hi], ALU.min, ALU.max)
+
+        def finish(t, lo=0, hi=S):
+            nc.vector.tensor_tensor(res[t][:, lo:hi], step[t][:, lo:hi], s_plain[t][:, lo:hi], ALU.add)
+            nc.sync.dma_start(out_rows[:, t, lo:hi], res[t][:, lo:hi])
+
+        fetch(da, n2_l, 0)
+        fetch(db, n3_l, 0)
+        for t in range(1, PACK):
+            fetch(da, n2_l, t)
+            clip_above(t - 1)
+            if t > 1:
+                finish(t - 2)
+            fetch(db, n3_l, t)
+            clip_below(t - 1)
+        last = PACK - 1
+        clip_above(last, 0, HALF)
+        finish(last - 1)
+        clip_above(last, HALF, S)
+        clip_below(last, 0, HALF)
+        clip_below(last, HALF, S)
+        finish(last, 0, HALF)
+        finish(last, HALF, S)

@@ -1,6 +1,7 @@
 from contextlib import ExitStack
 
 import concourse.mybir as mybir
+from concourse.masks import make_identity
 
 K, T, S, H, C = 512, 2048, 512, 512, 512
 FLOPS = 2 * K * H * S + 2 * K * C * S
@@ -20,7 +21,6 @@ PACK = 4
 LIST_ROWS = 16
 HALF = S // 2
 Z_CHUNKS = ((0, 256), (256, 384), (384, 512))
-W_SPLIT = 64
 
 
 def tile_picked_candtwicemed_none_p_kernel(
@@ -65,9 +65,8 @@ def tile_picked_candtwicemed_none_p_kernel(
         w_bf = keep.tile([P, PACK, P, PACK], BF16, name="w_bf", align_bytes=64)
         w_dst = w_bf[:].rearrange("p t m j -> p m j t")
         w_src = w_raw[:].rearrange("p j (m t) -> p m j t", t=PACK)
-        nc.scalar.copy(w_dst[:, W_SPLIT:P, :, 2:4], w_src[:, W_SPLIT:P, :, 2:4])
+        nc.scalar.copy(w_dst[:, :, :, 2:4], w_src[:, :, :, 2:4])
         nc.vector.tensor_copy(w_dst[:, :, :, 0:2], w_src[:, :, :, 0:2])
-        nc.vector.tensor_copy(w_dst[:, 0:W_SPLIT, :, 2:4], w_src[:, 0:W_SPLIT, :, 2:4])
         cand_scales = keep.tile([P, C], U8, name="cand_scales", align_bytes=64)
         nc.vector.tensor_copy(
             cand_scales[:].rearrange("p (t m) -> p m t", t=PACK),
@@ -104,10 +103,12 @@ def tile_picked_candtwicemed_none_p_kernel(
             )
             return acc
 
-        def twin_tiles(name):
-            windows = [keep.tile([P, S if t == 0 else 2 * S], F32, name=f"{name}_win{t}") for t in range(PACK)]
-            last = keep.tile([P, S], F32, name=f"{name}_last")
-            plains = [windows[t + 1][:, S : 2 * S] for t in range(PACK - 1)] + [last[:]]
+        def twin_tiles(name, wide):
+            windows = [keep.tile([P, 2 * S if t in wide else S], F32, name=f"{name}_win{t}") for t in range(PACK)]
+            plains = [
+                windows[t + 1][:, S : 2 * S] if t + 1 in wide else keep.tile([P, S], F32, name=f"{name}_plain{t}")[:]
+                for t in range(PACK)
+            ]
             return windows, plains
 
         def leave_psum(acc, window, plain, lo, hi, scale):
@@ -115,36 +116,58 @@ def tile_picked_candtwicemed_none_p_kernel(
             nc.scalar.activation(plain[:, lo:hi], acc[:], COPY, scale=scale)
 
         def gather_minus(dst, window, lst, plain, lo, hi):
-            nc.vector.tensor_tensor(dst, window[:].indirect(entries(lst, lo, hi)), plain[:, lo:hi], ALU.subtract)
+            nc.vector.tensor_tensor(dst, window[:].indirect(entries(lst, lo, hi)), plain, ALU.subtract)
 
         def spans(t):
             return ((0, HALF), (HALF, S)) if t == 0 else ((0, S),)
 
-        y_win, y_plain = twin_tiles("y")
-        bank = 0
-        for t in range(PACK):
-            for lo, hi in spans(t):
-                acc = product(bank, w_codes, w_scales, t, xq_codes, xq_scales, lo, hi)
-                leave_psum(acc, y_win[t], y_plain[t], lo, hi, gain[:, t : t + 1])
-                bank = bank + 1
-
-        neg_st = [keep.tile([P, S], F32, name=f"neg_st{t}") for t in range(PACK)]
+        y_win, y_plain = twin_tiles("y", (1, 2))
+        last = PACK - 1
+        neg_st = [keep.tile([P, S], F32, name=f"neg_st{t}") for t in range(last)]
+        neg_st_last = [
+            keep.tile([P, hi - lo], F32, name=f"neg_st_last{c}", tag=f"z_after{c}", align_bytes=64)
+            for c, (lo, hi) in enumerate(Z_CHUNKS)
+        ]
         neg_half_st = [keep.tile([P, S], F32, name=f"neg_half_st{t}") for t in range(PACK)]
-        for t in range(PACK):
+
+        def project(t):
             for lo, hi in spans(t):
-                gather_minus(neg_st[t][:, lo:hi], y_win[t], n1_l, y_plain[t], lo, hi)
-            nc.scalar.activation(neg_half_st[t][:], neg_st[t][:], COPY, scale=0.5)
+                acc = product(t + (lo == 0 and t == 0) * PACK, w_codes, w_scales, t, xq_codes, xq_scales, lo, hi)
+                leave_psum(acc, y_win[t], y_plain[t], lo, hi, gain[:, t : t + 1])
+
+        def first_difference(t):
+            if t < last:
+                for lo, hi in spans(t):
+                    gather_minus(neg_st[t][:, lo:hi], y_win[t], n1_l, y_plain[t][:, lo:hi], lo, hi)
+                nc.scalar.activation(neg_half_st[t][:], neg_st[t][:], COPY, scale=0.5)
+            else:
+                for c, (lo, hi) in enumerate(Z_CHUNKS):
+                    gather_minus(neg_st_last[c][:], y_win[t], n1_l, y_plain[t][:, lo:hi], lo, hi)
+                    nc.scalar.activation(neg_half_st[t][:, lo:hi], neg_st_last[c][:], COPY, scale=0.5)
+
+        project(0)
+        for t in range(1, PACK):
+            project(t)
+            first_difference(t - 1)
+        first_difference(last)
 
         z_codes = keep.tile([P, S], U32, name="z_codes", align_bytes=64)
         z_scales = keep.tile([P, S], U8, name="z_scales", align_bytes=64)
-        s_win, s_plain = twin_tiles("s")
-        z_f32 = [keep.tile([P, PACK, hi - lo], F32, name=f"z_f32_{lo}") for lo, hi in Z_CHUNKS]
-        z_bf = [keep.tile([P, hi - lo, PACK], BF16, name=f"z_bf_{lo}", align_bytes=64) for lo, hi in Z_CHUNKS]
+        s_win, s_plain = twin_tiles("s", (1, 2, 3))
+        z_bf = [
+            keep.tile([P, hi - lo, PACK], BF16, name=f"z_bf_{c}", tag=f"z_bf_{c}", align_bytes=64)
+            for c, (lo, hi) in enumerate(Z_CHUNKS)
+        ]
+        z_f32 = [
+            keep.tile([P, PACK, hi - lo], F32, name=f"z_f32_{c}", tag=("z_first", "z_after0", "z_bf_0")[c], align_bytes=64)
+            for c, (lo, hi) in enumerate(Z_CHUNKS)
+        ]
 
         def z_gather(c):
             lo, hi = Z_CHUNKS[c]
             for t in range(PACK):
-                gather_minus(z_f32[c][:, t, :], neg_half_st[t], n1_l, neg_st[t], lo, hi)
+                plain = neg_st[t][:, lo:hi] if t < last else neg_st_last[c][:]
+                gather_minus(z_f32[c][:, t, :], neg_half_st[t], n1_l, plain, lo, hi)
 
         def z_round(c, copy):
             copy(
@@ -173,14 +196,14 @@ def tile_picked_candtwicemed_none_p_kernel(
         z_gather(2)
         z_quantize(1)
         scores(6, 0, *Z_CHUNKS[1])
-        scores(0, 1, *Z_CHUNKS[0])
-        scores(1, 1, *Z_CHUNKS[1])
+        scores(4, 1, *Z_CHUNKS[0])
+        scores(0, 1, *Z_CHUNKS[1])
         z_round(2, nc.vector.tensor_copy)
         z_quantize(2)
         scores(7, 0, *Z_CHUNKS[2])
-        scores(2, 1, *Z_CHUNKS[2])
-        scores(3, 2, 0, S)
-        scores(4, 3, 0, S)
+        scores(1, 1, *Z_CHUNKS[2])
+        scores(2, 2, 0, S)
+        scores(3, 3, 0, S)
 
         out_rows = out.rearrange("(p t) n -> p t n", t=PACK)
         da = [keep.tile([P, S], F32, name=f"da{t}") for t in range(PACK)]
@@ -189,9 +212,12 @@ def tile_picked_candtwicemed_none_p_kernel(
         step = [keep.tile([P, S], F32, name=f"step{t}") for t in range(PACK)]
         res = [keep.tile([P, S], F32, name=f"res{t}") for t in range(PACK)]
 
-        def fetch(dst, lst, t):
-            for lo, hi in spans(t):
-                gather_minus(dst[t][:, lo:hi], s_win[t], lst, s_plain[t], lo, hi)
+        turned = [keep.tile([P, S], F32, name=f"turned{t}") for t in range(last)]
+        identity = keep.tile([P, P], F32, name="identity")
+        make_identity(nc, identity[:])
+
+        def fetch(dst, lst, t, lo=0, hi=S):
+            gather_minus(dst[t][:, lo:hi], s_win[t], lst, s_plain[t][:, lo:hi], lo, hi)
 
         def clip_above(t, lo=0, hi=S):
             nc.vector.scalar_tensor_tensor(upper[t][:, lo:hi], da[t][:, lo:hi], 0.0, db[t][:, lo:hi], ALU.max, ALU.min)
@@ -199,24 +225,49 @@ def tile_picked_candtwicemed_none_p_kernel(
         def clip_below(t, lo=0, hi=S):
             nc.vector.scalar_tensor_tensor(step[t][:, lo:hi], da[t][:, lo:hi], 0.0, upper[t][:, lo:hi], ALU.min, ALU.max)
 
-        def finish(t, lo=0, hi=S):
+        def finish_on_vector(t, lo, hi):
             nc.vector.tensor_tensor(res[t][:, lo:hi], step[t][:, lo:hi], s_plain[t][:, lo:hi], ALU.add)
             nc.sync.dma_start(out_rows[:, t, lo:hi], res[t][:, lo:hi])
 
-        fetch(da, n2_l, 0)
-        fetch(db, n3_l, 0)
-        for t in range(1, PACK):
-            fetch(da, n2_l, t)
-            clip_above(t - 1)
-            if t > 1:
-                finish(t - 2)
-            fetch(db, n3_l, t)
-            clip_below(t - 1)
-        last = PACK - 1
-        clip_above(last, 0, HALF)
-        finish(last - 1)
-        clip_above(last, HALF, S)
-        clip_below(last, 0, HALF)
-        clip_below(last, HALF, S)
-        finish(last, 0, HALF)
-        finish(last, HALF, S)
+        def finish_on_tensor(t, bank_sum, bank_back):
+            total = psum.tile([P, S], F32, name=f"total{t}", tag=f"bank{bank_sum}")
+            for lo in range(0, S, P):
+                cols = slice(lo, lo + P)
+                nc.tensor.matmul(total[:, cols], s_plain[t][:, cols], identity[:], start=True, stop=False, is_transpose=True)
+                nc.tensor.matmul(total[:, cols], step[t][:, cols], identity[:], start=False, stop=True, is_transpose=True)
+            nc.scalar.copy(turned[t][:], total[:])
+            back = psum.tile([P, S], F32, name=f"back{t}", tag=f"bank{bank_back}")
+            for lo in range(0, S, P):
+                cols = slice(lo, lo + P)
+                nc.tensor.transpose(back[:, cols], turned[t][:, cols], identity[:])
+            nc.scalar.copy(res[t][:], back[:])
+            nc.sync.dma_start(out_rows[:, t, :], res[t][:])
+
+        halves = ((0, HALF), (HALF, S))
+
+        def by_halves(stage, *args):
+            for lo, hi in halves:
+                stage(*args, lo, hi)
+
+        by_halves(fetch, da, n2_l, 0)
+        by_halves(fetch, db, n3_l, 0)
+        fetch(da, n2_l, 1, 0, HALF)
+        clip_above(0)
+        fetch(da, n2_l, 1, HALF, S)
+        clip_below(0)
+        finish_on_tensor(0, 5, 6)
+        fetch(db, n3_l, 1)
+        fetch(da, n2_l, 2, 0, HALF)
+        clip_above(1)
+        fetch(da, n2_l, 2, HALF, S)
+        clip_below(1)
+        finish_on_tensor(1, 5, 6)
+        by_halves(fetch, db, n3_l, 2)
+        by_halves(clip_above, 2)
+        by_halves(clip_below, 2)
+        finish_on_tensor(2, 5, 6)
+        fetch(da, n2_l, 3)
+        by_halves(fetch, db, n3_l, 3)
+        by_halves(clip_above, 3)
+        by_halves(clip_below, 3)
+        by_halves(finish_on_vector, 3)

@@ -15,6 +15,7 @@ U8 = mybir.dt.uint8
 FP8X4 = mybir.dt.float8_e4m3fn_x4
 ALU = mybir.AluOpType
 COPY = mybir.ActivationFunctionType.Copy
+RELU = mybir.ActivationFunctionType.Relu
 
 P = 128
 PACK = 4
@@ -62,11 +63,10 @@ def tile_picked_candtwicemed_none_p_kernel(
         cand_scales_listed = keep.tile([P, C], U8, name="cand_scales_listed", align_bytes=64)
         nc.vector.tensor_copy(cand_scales_listed[:], scale_table[:].indirect(cand_l[:]))
 
-        w_bf = keep.tile([P, PACK, P, PACK], BF16, name="w_bf", align_bytes=64)
-        w_dst = w_bf[:].rearrange("p t m j -> p m j t")
         w_src = w_raw[:].rearrange("p j (m t) -> p m j t", t=PACK)
-        nc.scalar.copy(w_dst[:, :, :, 2:4], w_src[:, :, :, 2:4])
-        nc.vector.tensor_copy(w_dst[:, :, :, 0:2], w_src[:, :, :, 0:2])
+        w_bf = [keep.tile([P, 2, P, PACK], BF16, name=f"w_bf{u}", tag=f"w_bf{u}", align_bytes=64) for u in range(2)]
+        nc.scalar.copy(w_bf[1][:].rearrange("p t m j -> p m j t"), w_src[:, :, :, 2:4])
+        nc.vector.tensor_copy(w_bf[0][:].rearrange("p t m j -> p m j t"), w_src[:, :, :, 0:2])
         cand_scales = keep.tile([P, C], U8, name="cand_scales", align_bytes=64)
         nc.vector.tensor_copy(
             cand_scales[:].rearrange("p (t m) -> p m t", t=PACK),
@@ -74,20 +74,21 @@ def tile_picked_candtwicemed_none_p_kernel(
         )
         w_codes = keep.tile([P, H], U32, name="w_codes", align_bytes=64)
         w_scales = keep.tile([P, H], U8, name="w_scales", align_bytes=64)
-        for t in (0, 2):
-            cols = slice(t * P, (t + 2) * P)
+        for u in range(2):
+            cols = slice(2 * u * P, 2 * (u + 1) * P)
             nc.vector.quantize_mx(
                 out=w_codes[:, cols].bitcast(FP8X4),
                 scales=w_scales[:, cols],
-                in_=w_bf[:, t : t + 2].rearrange("p t m j -> p (t m j)"),
+                in_=w_bf[u][:].rearrange("p t m j -> p (t m j)"),
             )
 
         words = word_table[:].bitcast(U32)
-        xq_codes = keep.tile([P, S], U32, name="xq_codes", align_bytes=64)
+        picked_codes = keep.tile([P, S + C], U32, name="picked_codes", tag="w_bf1", align_bytes=64)
+        xq_codes = picked_codes[:, 0:S]
         for lo in (0, HALF):
             nc.vector.tensor_copy(xq_codes[:, lo : lo + HALF], words.indirect(entries(offs_l, lo, lo + HALF)))
-        cand_codes = keep.tile([P, C], U32, name="cand_codes", align_bytes=64)
-        nc.vector.tensor_copy(cand_codes[:].rearrange("p (t m) -> p m t", t=PACK), words.indirect(cand_l[:]))
+        cand_codes = picked_codes[:, S : S + C]
+        nc.vector.tensor_copy(cand_codes.rearrange("p (t m) -> p m t", t=PACK), words.indirect(cand_l[:]))
 
         def product(bank, lhs_codes, lhs_scales, t, rhs_codes, rhs_scales, lo, hi):
             acc = psum.tile([P, hi - lo], F32, name=f"acc{bank}", tag=f"bank{bank}")
@@ -111,39 +112,35 @@ def tile_picked_candtwicemed_none_p_kernel(
             ]
             return windows, plains
 
-        def leave_psum(acc, window, plain, lo, hi, scale):
-            nc.scalar.activation(window[:, lo:hi], acc[:], COPY, scale=scale)
-            nc.scalar.activation(plain[:, lo:hi], acc[:], COPY, scale=scale)
+        def leave_psum(acc, window, plain, lo, hi, window_scale, plain_scale):
+            nc.scalar.activation(window[:, lo:hi], acc[:], COPY, scale=window_scale)
+            nc.scalar.activation(plain[:, lo:hi], acc[:], COPY, scale=plain_scale)
 
-        def gather_minus(dst, window, lst, plain, lo, hi):
-            nc.vector.tensor_tensor(dst, window[:].indirect(entries(lst, lo, hi)), plain, ALU.subtract)
+        def gather_with(dst, window, lst, plain, op, lo, hi):
+            nc.vector.tensor_tensor(dst, window[:].indirect(entries(lst, lo, hi)), plain, op)
 
-        def spans(t):
-            return ((0, HALF), (HALF, S)) if t == 0 else ((0, S),)
-
-        y_win, y_plain = twin_tiles("y", (1, 2))
         last = PACK - 1
+        halves = ((0, HALF), (HALF, S))
+        y_win, y_plain = twin_tiles("y", (1, 2))
         neg_st = [keep.tile([P, S], F32, name=f"neg_st{t}") for t in range(last)]
-        neg_st_last = [
-            keep.tile([P, hi - lo], F32, name=f"neg_st_last{c}", tag=f"z_after{c}", align_bytes=64)
-            for c, (lo, hi) in enumerate(Z_CHUNKS)
-        ]
+        neg_st_last = [keep.tile([P, HALF], F32, name=f"neg_st_last{h}", tag=f"neg_st_last{h}", align_bytes=64) for h in range(2)]
         neg_half_st = [keep.tile([P, S], F32, name=f"neg_half_st{t}") for t in range(PACK)]
 
+        def neg_st_at(t, lo, hi):
+            if t < last:
+                return neg_st[t][:, lo:hi]
+            return neg_st_last[lo // HALF][:, lo % HALF : lo % HALF + hi - lo]
+
         def project(t):
-            for lo, hi in spans(t):
+            for lo, hi in halves if t == 0 else ((0, S),):
                 acc = product(t + (lo == 0 and t == 0) * PACK, w_codes, w_scales, t, xq_codes, xq_scales, lo, hi)
-                leave_psum(acc, y_win[t], y_plain[t], lo, hi, gain[:, t : t + 1])
+                leave_psum(acc, y_win[t], y_plain[t], lo, hi, gain[:, t : t + 1], gain[:, t : t + 1])
 
         def first_difference(t):
-            if t < last:
-                for lo, hi in spans(t):
-                    gather_minus(neg_st[t][:, lo:hi], y_win[t], n1_l, y_plain[t][:, lo:hi], lo, hi)
-                nc.scalar.activation(neg_half_st[t][:], neg_st[t][:], COPY, scale=0.5)
-            else:
-                for c, (lo, hi) in enumerate(Z_CHUNKS):
-                    gather_minus(neg_st_last[c][:], y_win[t], n1_l, y_plain[t][:, lo:hi], lo, hi)
-                    nc.scalar.activation(neg_half_st[t][:, lo:hi], neg_st_last[c][:], COPY, scale=0.5)
+            for lo, hi in halves if t in (0, last) else ((0, S),):
+                gather_with(neg_st_at(t, lo, hi), y_win[t], n1_l, y_plain[t][:, lo:hi], ALU.subtract, lo, hi)
+            for lo, hi in halves if t == last else ((0, S),):
+                nc.scalar.activation(neg_half_st[t][:, lo:hi], neg_st_at(t, lo, hi), COPY, scale=0.5)
 
         project(0)
         for t in range(1, PACK):
@@ -153,121 +150,132 @@ def tile_picked_candtwicemed_none_p_kernel(
 
         z_codes = keep.tile([P, S], U32, name="z_codes", align_bytes=64)
         z_scales = keep.tile([P, S], U8, name="z_scales", align_bytes=64)
-        s_win, s_plain = twin_tiles("s", (1, 2, 3))
-        z_bf = [
-            keep.tile([P, hi - lo, PACK], BF16, name=f"z_bf_{c}", tag=f"z_bf_{c}", align_bytes=64)
-            for c, (lo, hi) in enumerate(Z_CHUNKS)
-        ]
+        s_win, neg_s = twin_tiles("s", (1, 2, 3))
+        shared = keep.tile([P, 896], F32, name="shared", tag="neg_st_last0", align_bytes=64)
         z_f32 = [
-            keep.tile([P, PACK, hi - lo], F32, name=f"z_f32_{c}", tag=("z_first", "z_after0", "z_bf_0")[c], align_bytes=64)
-            for c, (lo, hi) in enumerate(Z_CHUNKS)
+            keep.tile([P, PACK * 256], F32, name="z_f32_0")[:],
+            keep.tile([P, PACK * 128], F32, name="z_f32_1")[:],
+            shared[:, 0:512],
+        ]
+        z_bf = [
+            shared[:, 384:896].bitcast(BF16),
+            keep.tile([P, PACK * 128], BF16, name="z_bf_1", align_bytes=64)[:],
+            keep.tile([P, PACK * 128], BF16, name="z_bf_2", align_bytes=64)[:],
         ]
 
-        def z_gather(c):
+        def z_gather(c, t):
             lo, hi = Z_CHUNKS[c]
-            for t in range(PACK):
-                plain = neg_st[t][:, lo:hi] if t < last else neg_st_last[c][:]
-                gather_minus(z_f32[c][:, t, :], neg_half_st[t], n1_l, plain, lo, hi)
+            dst = z_f32[c][:, t * (hi - lo) : (t + 1) * (hi - lo)]
+            gather_with(dst, neg_half_st[t], n1_l, neg_st_at(t, lo, hi), ALU.subtract, lo, hi)
 
         def z_round(c, copy):
             copy(
-                z_bf[c][:].rearrange("p (c i) t -> p c t i", i=4),
-                z_f32[c][:].rearrange("p t (c i) -> p c t i", i=4),
+                z_bf[c].rearrange("p (c i t) -> p c t i", i=4, t=PACK),
+                z_f32[c].rearrange("p (t c i) -> p c t i", i=4, t=PACK),
             )
 
         def z_quantize(c):
             lo, hi = Z_CHUNKS[c]
-            nc.vector.quantize_mx(
-                out=z_codes[:, lo:hi].bitcast(FP8X4),
-                scales=z_scales[:, lo:hi],
-                in_=z_bf[c][:].rearrange("p n t -> p (n t)"),
-            )
+            nc.vector.quantize_mx(out=z_codes[:, lo:hi].bitcast(FP8X4), scales=z_scales[:, lo:hi], in_=z_bf[c])
 
         def scores(bank, t, lo, hi):
             acc = product(bank, cand_codes, cand_scales, t, z_codes, z_scales, lo, hi)
-            leave_psum(acc, s_win[t], s_plain[t], lo, hi, 0.0625)
+            leave_psum(acc, s_win[t], neg_s[t], lo, hi, 0.0625, -0.0625)
 
-        z_gather(0)
+        for t in range(PACK):
+            z_gather(0, t)
+            z_gather(1, t)
         z_round(0, nc.scalar.copy)
-        z_gather(1)
         z_round(1, nc.scalar.copy)
+        for t in range(last):
+            z_gather(2, t)
         z_quantize(0)
         scores(5, 0, *Z_CHUNKS[0])
-        z_gather(2)
+        z_gather(2, last)
         z_quantize(1)
         scores(6, 0, *Z_CHUNKS[1])
-        scores(4, 1, *Z_CHUNKS[0])
-        scores(0, 1, *Z_CHUNKS[1])
         z_round(2, nc.vector.tensor_copy)
         z_quantize(2)
         scores(7, 0, *Z_CHUNKS[2])
-        scores(1, 1, *Z_CHUNKS[2])
-        scores(2, 2, 0, S)
-        scores(3, 3, 0, S)
+        scores(1, 1, 0, S)
 
         out_rows = out.rearrange("(p t) n -> p t n", t=PACK)
         da = [keep.tile([P, S], F32, name=f"da{t}") for t in range(PACK)]
         db = [keep.tile([P, S], F32, name=f"db{t}") for t in range(PACK)]
         upper = [keep.tile([P, S], F32, name=f"upper{t}") for t in range(PACK)]
-        step = [keep.tile([P, S], F32, name=f"step{t}") for t in range(PACK)]
         res = [keep.tile([P, S], F32, name=f"res{t}") for t in range(PACK)]
-
-        turned = [keep.tile([P, S], F32, name=f"turned{t}") for t in range(last)]
         identity = keep.tile([P, P], F32, name="identity")
         make_identity(nc, identity[:])
 
         def fetch(dst, lst, t, lo=0, hi=S):
-            gather_minus(dst[t][:, lo:hi], s_win[t], lst, s_plain[t][:, lo:hi], lo, hi)
+            gather_with(dst[t][:, lo:hi], s_win[t], lst, neg_s[t][:, lo:hi], ALU.add, lo, hi)
 
         def clip_above(t, lo=0, hi=S):
             nc.vector.scalar_tensor_tensor(upper[t][:, lo:hi], da[t][:, lo:hi], 0.0, db[t][:, lo:hi], ALU.max, ALU.min)
 
-        def clip_below(t, lo=0, hi=S):
-            nc.vector.scalar_tensor_tensor(step[t][:, lo:hi], da[t][:, lo:hi], 0.0, upper[t][:, lo:hi], ALU.min, ALU.max)
+        def clip_below(step, t, lo, hi):
+            nc.vector.scalar_tensor_tensor(step[:, lo:hi], da[t][:, lo:hi], 0.0, upper[t][:, lo:hi], ALU.min, ALU.max)
 
-        def finish_on_vector(t, lo, hi):
-            nc.vector.tensor_tensor(res[t][:, lo:hi], step[t][:, lo:hi], s_plain[t][:, lo:hi], ALU.add)
-            nc.sync.dma_start(out_rows[:, t, lo:hi], res[t][:, lo:hi])
-
-        def finish_on_tensor(t, bank_sum, bank_back):
-            total = psum.tile([P, S], F32, name=f"total{t}", tag=f"bank{bank_sum}")
-            for lo in range(0, S, P):
-                cols = slice(lo, lo + P)
-                nc.tensor.matmul(total[:, cols], s_plain[t][:, cols], identity[:], start=True, stop=False, is_transpose=True)
-                nc.tensor.matmul(total[:, cols], step[t][:, cols], identity[:], start=False, stop=True, is_transpose=True)
-            nc.scalar.copy(turned[t][:], total[:])
-            back = psum.tile([P, S], F32, name=f"back{t}", tag=f"bank{bank_back}")
-            for lo in range(0, S, P):
-                cols = slice(lo, lo + P)
-                nc.tensor.transpose(back[:, cols], turned[t][:, cols], identity[:])
-            nc.scalar.copy(res[t][:], back[:])
-            nc.sync.dma_start(out_rows[:, t, :], res[t][:])
-
-        halves = ((0, HALF), (HALF, S))
+        def turned_sum(dst, bank, terms, lo, hi, func=COPY, scale=1.0):
+            total = psum.tile([P, hi - lo], F32, name=f"total{bank}", tag=f"bank{bank}")
+            for at in range(lo, hi, P):
+                for n, term in enumerate(terms):
+                    nc.tensor.matmul(
+                        total[:, at - lo : at - lo + P],
+                        term[:, at : at + P],
+                        identity[:],
+                        start=n == 0,
+                        stop=n == len(terms) - 1,
+                        is_transpose=True,
+                    )
+            nc.scalar.activation(dst[:, lo:hi], total[:], func, scale=scale)
 
         def by_halves(stage, *args):
             for lo, hi in halves:
                 stage(*args, lo, hi)
 
+        def lower_end(t):
+            drop = keep.tile([P, S], F32, name=f"drop{t}")
+            nc.scalar.activation(drop[:], da[t][:], RELU, scale=-1.0)
+            low = keep.tile([P, S], F32, name=f"low{t}")
+            turned_sum(low, 4, (neg_s[t], drop), 0, S, scale=-1.0)
+            rise = keep.tile([P, S], F32, name=f"rise{t}")
+            return drop, low, rise
+
+        def rise_on_tensor(t, drop, low, rise, lo=0, hi=S):
+            turned_sum(rise, 5 + lo // HALF * 2, (drop, upper[t]), lo, hi, RELU)
+
+        def finish_on_tensor(t, drop, low, rise, lo=0, hi=S):
+            turned_sum(res[t], 6 - lo // HALF * 6, (low, rise), lo, hi)
+            nc.scalar.dma_start(out_rows[:, t, lo:hi], res[t][:, lo:hi])
+
+        def finish_on_vector(step, t, lo, hi):
+            nc.vector.tensor_tensor(res[t][:, lo:hi], step[:, lo:hi], neg_s[t][:, lo:hi], ALU.subtract)
+            nc.sync.dma_start(out_rows[:, t, lo:hi], res[t][:, lo:hi])
+
         by_halves(fetch, da, n2_l, 0)
+        ends0 = lower_end(0)
+        scores(2, 2, 0, S)
         by_halves(fetch, db, n3_l, 0)
-        fetch(da, n2_l, 1, 0, HALF)
+        fetch(da, n2_l, 1)
         clip_above(0)
-        fetch(da, n2_l, 1, HALF, S)
-        clip_below(0)
-        finish_on_tensor(0, 5, 6)
+        rise_on_tensor(0, *ends0)
+        finish_on_tensor(0, *ends0)
+        ends1 = lower_end(1)
+        scores(3, 3, 0, S)
         fetch(db, n3_l, 1)
-        fetch(da, n2_l, 2, 0, HALF)
+        fetch(da, n2_l, 2)
         clip_above(1)
-        fetch(da, n2_l, 2, HALF, S)
-        clip_below(1)
-        finish_on_tensor(1, 5, 6)
+        rise_on_tensor(1, *ends1)
+        finish_on_tensor(1, *ends1)
+        ends2 = lower_end(2)
         by_halves(fetch, db, n3_l, 2)
         by_halves(clip_above, 2)
-        by_halves(clip_below, 2)
-        finish_on_tensor(2, 5, 6)
+        by_halves(rise_on_tensor, 2, *ends2)
+        by_halves(finish_on_tensor, 2, *ends2)
         fetch(da, n2_l, 3)
         by_halves(fetch, db, n3_l, 3)
         by_halves(clip_above, 3)
-        by_halves(clip_below, 3)
-        by_halves(finish_on_vector, 3)
+        step3 = keep.tile([P, S], F32, name="step3")
+        by_halves(clip_below, step3, 3)
+        by_halves(finish_on_vector, step3, 3)

@@ -19,9 +19,15 @@ RELU = mybir.ActivationFunctionType.Relu
 
 P = 128
 PACK = 4
+LAST = PACK - 1
+QUADRANT = 32
 LIST_ROWS = 16
+LINE = 4
 HALF = S // 2
-Z_CHUNKS = ((0, 256), (256, 384), (384, 512))
+WHOLE = ((0, S),)
+HALVES = ((0, HALF), (HALF, S))
+Z_RANGES = ((0, 256), (256, 384), (384, 512))
+SCORE_SCALE = 0.0625
 
 
 def tile_picked_candtwicemed_none_p_kernel(
@@ -40,12 +46,17 @@ def tile_picked_candtwicemed_none_p_kernel(
         def entries(lst, lo, hi):
             return lst[:, lo // LIST_ROWS : hi // LIST_ROWS]
 
+        def by_halves(stage, *args):
+            for lo, hi in HALVES:
+                stage(*args, lo, hi)
+
         scale_table = keep.tile([P, T], U8, name="scale_table", align_bytes=64)
         offs_l = load_list(offs, "offs_l")
-        for q in range(4):
-            rows = x_scales[0, 4 * q : 4 * q + 4, :].bitcast(I32)
+        for q in range(P // QUADRANT):
+            rows = x_scales[0, PACK * q : PACK * (q + 1), :].bitcast(I32)
             nc.sync.dma_start(
-                scale_table[32 * q : 32 * q + 32, :].bitcast(I32), rows.unsqueeze(0).to_broadcast([8, 4, T // 4])
+                scale_table[QUADRANT * q : QUADRANT * (q + 1), :].bitcast(I32),
+                rows.unsqueeze(0).to_broadcast([QUADRANT // PACK, PACK, T // 4]),
             )
         cand_l = load_list(cand, "cand_l")
         w_raw = keep.tile([P, PACK, H], F32, name="w_raw")
@@ -64,7 +75,7 @@ def tile_picked_candtwicemed_none_p_kernel(
         nc.vector.tensor_copy(cand_scales_listed[:], scale_table[:].indirect(cand_l[:]))
 
         w_src = w_raw[:].rearrange("p j (m t) -> p m j t", t=PACK)
-        w_bf = [keep.tile([P, 2, P, PACK], BF16, name=f"w_bf{u}", tag=f"w_bf{u}", align_bytes=64) for u in range(2)]
+        w_bf = [keep.tile([P, 2, P, PACK], BF16, name=f"w_bf{u}", align_bytes=64) for u in range(2)]
         nc.scalar.copy(w_bf[1][:].rearrange("p t m j -> p m j t"), w_src[:, :, :, 2:4])
         nc.vector.tensor_copy(w_bf[0][:].rearrange("p t m j -> p m j t"), w_src[:, :, :, 0:2])
         cand_scales = keep.tile([P, C], U8, name="cand_scales", align_bytes=64)
@@ -83,10 +94,10 @@ def tile_picked_candtwicemed_none_p_kernel(
             )
 
         words = word_table[:].bitcast(U32)
-        picked_codes = keep.tile([P, S + C], U32, name="picked_codes", tag="w_bf1", align_bytes=64)
+        picked_codes = keep.tile([P, S + C], U32, name="picked_codes", align_bytes=64)
         xq_codes = picked_codes[:, 0:S]
-        for lo in (0, HALF):
-            nc.vector.tensor_copy(xq_codes[:, lo : lo + HALF], words.indirect(entries(offs_l, lo, lo + HALF)))
+        for lo, hi in HALVES:
+            nc.vector.tensor_copy(xq_codes[:, lo:hi], words.indirect(entries(offs_l, lo, hi)))
         cand_codes = picked_codes[:, S : S + C]
         nc.vector.tensor_copy(cand_codes.rearrange("p (t m) -> p m t", t=PACK), words.indirect(cand_l[:]))
 
@@ -119,84 +130,87 @@ def tile_picked_candtwicemed_none_p_kernel(
         def gather_with(dst, window, lst, plain, op, lo, hi):
             nc.vector.tensor_tensor(dst, window[:].indirect(entries(lst, lo, hi)), plain, op)
 
-        last = PACK - 1
-        halves = ((0, HALF), (HALF, S))
         y_win, y_plain = twin_tiles("y", (1, 2))
-        neg_st = [keep.tile([P, S], F32, name=f"neg_st{t}") for t in range(last)]
-        neg_st_last = [keep.tile([P, HALF], F32, name=f"neg_st_last{h}", tag=f"neg_st_last{h}", align_bytes=64) for h in range(2)]
+        neg_st = [keep.tile([P, S], F32, name=f"neg_st{t}") for t in range(LAST)]
+        neg_st_last = [
+            keep.tile([P, HALF], F32, name=f"neg_st_last{h}", tag=f"neg_st_last{h}", align_bytes=64) for h in range(2)
+        ]
         neg_half_st = [keep.tile([P, S], F32, name=f"neg_half_st{t}") for t in range(PACK)]
 
         def neg_st_at(t, lo, hi):
-            if t < last:
+            if t < LAST:
                 return neg_st[t][:, lo:hi]
             return neg_st_last[lo // HALF][:, lo % HALF : lo % HALF + hi - lo]
 
         def project(t):
-            for lo, hi in halves if t == 0 else ((0, S),):
-                acc = product(t + (lo == 0 and t == 0) * PACK, w_codes, w_scales, t, xq_codes, xq_scales, lo, hi)
+            for lo, hi in HALVES if t == 0 else WHOLE:
+                bank = PACK if (t, lo) == (0, 0) else t
+                acc = product(bank, w_codes, w_scales, t, xq_codes, xq_scales, lo, hi)
                 leave_psum(acc, y_win[t], y_plain[t], lo, hi, gain[:, t : t + 1], gain[:, t : t + 1])
 
         def first_difference(t):
-            for lo, hi in halves if t in (0, last) else ((0, S),):
+            for lo, hi in HALVES if t in (0, LAST) else WHOLE:
                 gather_with(neg_st_at(t, lo, hi), y_win[t], n1_l, y_plain[t][:, lo:hi], ALU.subtract, lo, hi)
-            for lo, hi in halves if t == last else ((0, S),):
+            for lo, hi in HALVES if t == LAST else WHOLE:
                 nc.scalar.activation(neg_half_st[t][:, lo:hi], neg_st_at(t, lo, hi), COPY, scale=0.5)
 
         project(0)
         for t in range(1, PACK):
             project(t)
             first_difference(t - 1)
-        first_difference(last)
+        first_difference(LAST)
 
         z_codes = keep.tile([P, S], U32, name="z_codes", align_bytes=64)
         z_scales = keep.tile([P, S], U8, name="z_scales", align_bytes=64)
         s_win, neg_s = twin_tiles("s", (1, 2, 3))
-        shared = keep.tile([P, 896], F32, name="shared", tag="neg_st_last0", align_bytes=64)
+        z_sizes = [PACK * (hi - lo) for lo, hi in Z_RANGES]
+        overlap_at = z_sizes[2] // PACK * LAST
+        reused = keep.tile([P, overlap_at + z_sizes[0] // 2], F32, name="reused", tag="neg_st_last0", align_bytes=64)
         z_f32 = [
-            keep.tile([P, PACK * 256], F32, name="z_f32_0")[:],
-            keep.tile([P, PACK * 128], F32, name="z_f32_1")[:],
-            shared[:, 0:512],
+            keep.tile([P, z_sizes[0]], F32, name="z_f32_0")[:],
+            keep.tile([P, z_sizes[1]], F32, name="z_f32_1")[:],
+            reused[:, 0 : z_sizes[2]],
         ]
         z_bf = [
-            shared[:, 384:896].bitcast(BF16),
-            keep.tile([P, PACK * 128], BF16, name="z_bf_1", align_bytes=64)[:],
-            keep.tile([P, PACK * 128], BF16, name="z_bf_2", align_bytes=64)[:],
+            reused[:, overlap_at : overlap_at + z_sizes[0] // 2].bitcast(BF16),
+            keep.tile([P, z_sizes[1]], BF16, name="z_bf_1", align_bytes=64)[:],
+            keep.tile([P, z_sizes[2]], BF16, name="z_bf_2", align_bytes=64)[:],
         ]
 
-        def z_gather(c, t):
-            lo, hi = Z_CHUNKS[c]
-            dst = z_f32[c][:, t * (hi - lo) : (t + 1) * (hi - lo)]
+        def z_gather(r, t):
+            lo, hi = Z_RANGES[r]
+            dst = z_f32[r][:, t * (hi - lo) : (t + 1) * (hi - lo)]
             gather_with(dst, neg_half_st[t], n1_l, neg_st_at(t, lo, hi), ALU.subtract, lo, hi)
 
-        def z_round(c, copy):
+        def z_round(r, copy):
             copy(
-                z_bf[c].rearrange("p (c i t) -> p c t i", i=4, t=PACK),
-                z_f32[c].rearrange("p (t c i) -> p c t i", i=4, t=PACK),
+                z_bf[r].rearrange("p (c i t) -> p c t i", i=LINE, t=PACK),
+                z_f32[r].rearrange("p (t c i) -> p c t i", i=LINE, t=PACK),
             )
 
-        def z_quantize(c):
-            lo, hi = Z_CHUNKS[c]
-            nc.vector.quantize_mx(out=z_codes[:, lo:hi].bitcast(FP8X4), scales=z_scales[:, lo:hi], in_=z_bf[c])
+        def z_quantize(r):
+            lo, hi = Z_RANGES[r]
+            nc.vector.quantize_mx(out=z_codes[:, lo:hi].bitcast(FP8X4), scales=z_scales[:, lo:hi], in_=z_bf[r])
 
         def scores(bank, t, lo, hi):
             acc = product(bank, cand_codes, cand_scales, t, z_codes, z_scales, lo, hi)
-            leave_psum(acc, s_win[t], neg_s[t], lo, hi, 0.0625, -0.0625)
+            leave_psum(acc, s_win[t], neg_s[t], lo, hi, SCORE_SCALE, -SCORE_SCALE)
 
         for t in range(PACK):
             z_gather(0, t)
             z_gather(1, t)
         z_round(0, nc.scalar.copy)
         z_round(1, nc.scalar.copy)
-        for t in range(last):
+        for t in range(LAST):
             z_gather(2, t)
         z_quantize(0)
-        scores(5, 0, *Z_CHUNKS[0])
-        z_gather(2, last)
+        scores(5, 0, *Z_RANGES[0])
+        z_gather(2, LAST)
         z_quantize(1)
-        scores(6, 0, *Z_CHUNKS[1])
+        scores(6, 0, *Z_RANGES[1])
         z_round(2, nc.vector.tensor_copy)
         z_quantize(2)
-        scores(7, 0, *Z_CHUNKS[2])
+        scores(7, 0, *Z_RANGES[2])
         scores(1, 1, 0, S)
 
         out_rows = out.rearrange("(p t) n -> p t n", t=PACK)
@@ -216,38 +230,32 @@ def tile_picked_candtwicemed_none_p_kernel(
         def clip_below(step, t, lo, hi):
             nc.vector.scalar_tensor_tensor(step[:, lo:hi], da[t][:, lo:hi], 0.0, upper[t][:, lo:hi], ALU.min, ALU.max)
 
-        def turned_sum(dst, bank, terms, lo, hi, func=COPY, scale=1.0):
-            total = psum.tile([P, hi - lo], F32, name=f"total{bank}", tag=f"bank{bank}")
-            for at in range(lo, hi, P):
+        def turned_sum(dst, bank, terms, func=COPY, scale=1.0):
+            total = psum.tile([P, S], F32, name=f"total{bank}", tag=f"bank{bank}")
+            for at in range(0, S, P):
                 for n, term in enumerate(terms):
                     nc.tensor.matmul(
-                        total[:, at - lo : at - lo + P],
+                        total[:, at : at + P],
                         term[:, at : at + P],
                         identity[:],
                         start=n == 0,
                         stop=n == len(terms) - 1,
                         is_transpose=True,
                     )
-            nc.scalar.activation(dst[:, lo:hi], total[:], func, scale=scale)
-
-        def by_halves(stage, *args):
-            for lo, hi in halves:
-                stage(*args, lo, hi)
+            nc.scalar.activation(dst[:], total[:], func, scale=scale)
 
         def lower_end(t):
             drop = keep.tile([P, S], F32, name=f"drop{t}")
             nc.scalar.activation(drop[:], da[t][:], RELU, scale=-1.0)
             low = keep.tile([P, S], F32, name=f"low{t}")
-            turned_sum(low, 4, (neg_s[t], drop), 0, S, scale=-1.0)
+            turned_sum(low, 4, (neg_s[t], drop), scale=-1.0)
+            return drop, low
+
+        def finish_on_tensor(t, drop, low):
             rise = keep.tile([P, S], F32, name=f"rise{t}")
-            return drop, low, rise
-
-        def rise_on_tensor(t, drop, low, rise, lo=0, hi=S):
-            turned_sum(rise, 5 + lo // HALF * 2, (drop, upper[t]), lo, hi, RELU)
-
-        def finish_on_tensor(t, drop, low, rise, lo=0, hi=S):
-            turned_sum(res[t], 6 - lo // HALF * 6, (low, rise), lo, hi)
-            nc.scalar.dma_start(out_rows[:, t, lo:hi], res[t][:, lo:hi])
+            turned_sum(rise, 5, (drop, upper[t]), RELU)
+            turned_sum(res[t], 6, (low, rise))
+            nc.scalar.dma_start(out_rows[:, t, :], res[t][:])
 
         def finish_on_vector(step, t, lo, hi):
             nc.vector.tensor_tensor(res[t][:, lo:hi], step[:, lo:hi], neg_s[t][:, lo:hi], ALU.subtract)
@@ -259,23 +267,18 @@ def tile_picked_candtwicemed_none_p_kernel(
         by_halves(fetch, db, n3_l, 0)
         fetch(da, n2_l, 1)
         clip_above(0)
-        rise_on_tensor(0, *ends0)
         finish_on_tensor(0, *ends0)
         ends1 = lower_end(1)
         scores(3, 3, 0, S)
         fetch(db, n3_l, 1)
         fetch(da, n2_l, 2)
         clip_above(1)
-        rise_on_tensor(1, *ends1)
         finish_on_tensor(1, *ends1)
-        ends2 = lower_end(2)
-        by_halves(fetch, db, n3_l, 2)
-        by_halves(clip_above, 2)
-        by_halves(rise_on_tensor, 2, *ends2)
-        by_halves(finish_on_tensor, 2, *ends2)
-        fetch(da, n2_l, 3)
-        by_halves(fetch, db, n3_l, 3)
-        by_halves(clip_above, 3)
-        step3 = keep.tile([P, S], F32, name="step3")
-        by_halves(clip_below, step3, 3)
-        by_halves(finish_on_vector, step3, 3)
+        for t in (2, LAST):
+            by_halves(fetch, db, n3_l, t)
+            by_halves(clip_above, t)
+            step = keep.tile([P, S], F32, name=f"step{t}")
+            by_halves(clip_below, step, t)
+            by_halves(finish_on_vector, step, t)
+            if t < LAST:
+                fetch(da, n2_l, t + 1)

from contextlib import ExitStack

import concourse.mybir as mybir
from concourse.masks import make_identity

K, T, S, H, C = 512, 2048, 512, 512, 512
FLOPS = 2 * K * H * S + 2 * K * C * S

F32 = mybir.dt.float32
BF16 = mybir.dt.bfloat16
I32 = mybir.dt.int32
U32 = mybir.dt.uint32
U16 = mybir.dt.uint16
U8 = mybir.dt.uint8
FP8X4 = mybir.dt.float8_e4m3fn_x4
ALU = mybir.AluOpType
COPY = mybir.ActivationFunctionType.Copy
RELU = mybir.ActivationFunctionType.Relu

P = 128
PACK = 4
LAST = PACK - 1
QUADRANT = 32
LIST_ROWS = 16
LINE = 4
HALF = S // 2
WHOLE = ((0, S),)
HALVES = ((0, HALF), (HALF, S))
Z_RANGES = ((0, 256), (256, 384), (384, 512))
SCORE_SCALE = 0.0625


def tile_picked_candtwicemed_none_p_kernel(
    tc, x_words, x_scales, w1, gs, offs, n1, cand, n2, n3, out
):
    nc = tc.nc
    with ExitStack() as ctx:
        keep = ctx.enter_context(tc.tile_pool(name="keep", bufs=1))
        psum = ctx.enter_context(tc.psum_pool(name="psum", bufs=1))

        def load_list(src, name):
            tile = keep.tile([P, S // LIST_ROWS], U16, name=name)
            nc.sync.dma_start(tile[:], src)
            return tile

        def entries(lst, lo, hi):
            return lst[:, lo // LIST_ROWS : hi // LIST_ROWS]

        def by_halves(stage, *args):
            for lo, hi in HALVES:
                stage(*args, lo, hi)

        scale_table = keep.tile([P, T], U8, name="scale_table", align_bytes=64)
        offs_l = load_list(offs, "offs_l")
        for q in range(P // QUADRANT):
            rows = x_scales[0, PACK * q : PACK * (q + 1), :].bitcast(I32)
            nc.sync.dma_start(
                scale_table[QUADRANT * q : QUADRANT * (q + 1), :].bitcast(I32),
                rows.unsqueeze(0).to_broadcast([QUADRANT // PACK, PACK, T // 4]),
            )
        cand_l = load_list(cand, "cand_l")
        w_raw = keep.tile([P, PACK, H], F32, name="w_raw")
        nc.sync.dma_start(w_raw[:], w1.rearrange("(p j) c -> p j c", j=PACK))
        word_table = keep.tile([P, T], I32, name="word_table", align_bytes=64)
        nc.sync.dma_start(word_table[:], x_words[0].rearrange("p n r -> p (n r)").bitcast(I32))
        gain = keep.tile([P, PACK], F32, name="gain")
        nc.sync.dma_start(gain[:], gs.rearrange("(p t) o -> p (t o)", t=PACK))
        n1_l = load_list(n1, "n1_l")
        n2_l = load_list(n2, "n2_l")
        n3_l = load_list(n3, "n3_l")

        xq_scales = keep.tile([P, S], U8, name="xq_scales", align_bytes=64)
        nc.vector.tensor_copy(xq_scales[:], scale_table[:].indirect(offs_l[:]))
        cand_scales_listed = keep.tile([P, C], U8, name="cand_scales_listed", align_bytes=64)
        nc.vector.tensor_copy(cand_scales_listed[:], scale_table[:].indirect(cand_l[:]))

        w_src = w_raw[:].rearrange("p j (m t) -> p m j t", t=PACK)
        w_bf = [keep.tile([P, 2, P, PACK], BF16, name=f"w_bf{u}", align_bytes=64) for u in range(2)]
        nc.scalar.copy(w_bf[1][:].rearrange("p t m j -> p m j t"), w_src[:, :, :, 2:4])
        nc.vector.tensor_copy(w_bf[0][:].rearrange("p t m j -> p m j t"), w_src[:, :, :, 0:2])
        cand_scales = keep.tile([P, C], U8, name="cand_scales", align_bytes=64)
        nc.vector.tensor_copy(
            cand_scales[:].rearrange("p (t m) -> p m t", t=PACK),
            cand_scales_listed[:].rearrange("p (m t) -> p m t", t=PACK),
        )
        w_codes = keep.tile([P, H], U32, name="w_codes", align_bytes=64)
        w_scales = keep.tile([P, H], U8, name="w_scales", align_bytes=64)
        for u in range(2):
            cols = slice(2 * u * P, 2 * (u + 1) * P)
            nc.vector.quantize_mx(
                out=w_codes[:, cols].bitcast(FP8X4),
                scales=w_scales[:, cols],
                in_=w_bf[u][:].rearrange("p t m j -> p (t m j)"),
            )

        words = word_table[:].bitcast(U32)
        picked_codes = keep.tile([P, S + C], U32, name="picked_codes", align_bytes=64)
        xq_codes = picked_codes[:, 0:S]
        for lo, hi in HALVES:
            nc.vector.tensor_copy(xq_codes[:, lo:hi], words.indirect(entries(offs_l, lo, hi)))
        cand_codes = picked_codes[:, S : S + C]
        nc.vector.tensor_copy(cand_codes.rearrange("p (t m) -> p m t", t=PACK), words.indirect(cand_l[:]))

        def product(bank, lhs_codes, lhs_scales, t, rhs_codes, rhs_scales, lo, hi):
            acc = psum.tile([P, hi - lo], F32, name=f"acc{bank}", tag=f"bank{bank}")
            rows = slice(t * P, (t + 1) * P)
            nc.tensor.matmul_mx(
                out=acc[:],
                lhsT=lhs_codes[:, rows].bitcast(FP8X4),
                lhsT_scale=lhs_scales[:, rows],
                rhs=rhs_codes[:, lo:hi].bitcast(FP8X4),
                rhs_scale=rhs_scales[:, lo:hi],
                start=True,
                stop=True,
            )
            return acc

        def twin_tiles(name, wide):
            windows = [keep.tile([P, 2 * S if t in wide else S], F32, name=f"{name}_win{t}") for t in range(PACK)]
            plains = [
                windows[t + 1][:, S : 2 * S] if t + 1 in wide else keep.tile([P, S], F32, name=f"{name}_plain{t}")[:]
                for t in range(PACK)
            ]
            return windows, plains

        def leave_psum(acc, window, plain, lo, hi, window_scale, plain_scale):
            nc.scalar.activation(window[:, lo:hi], acc[:], COPY, scale=window_scale)
            nc.scalar.activation(plain[:, lo:hi], acc[:], COPY, scale=plain_scale)

        def gather_with(dst, window, lst, plain, op, lo, hi):
            nc.vector.tensor_tensor(dst, window[:].indirect(entries(lst, lo, hi)), plain, op)

        y_win, y_plain = twin_tiles("y", (1, 2))
        neg_st = [keep.tile([P, S], F32, name=f"neg_st{t}") for t in range(LAST)]
        neg_st_last = [
            keep.tile([P, HALF], F32, name=f"neg_st_last{h}", tag=f"neg_st_last{h}", align_bytes=64) for h in range(2)
        ]
        neg_half_st = [keep.tile([P, S], F32, name=f"neg_half_st{t}") for t in range(PACK)]

        def neg_st_at(t, lo, hi):
            if t < LAST:
                return neg_st[t][:, lo:hi]
            return neg_st_last[lo // HALF][:, lo % HALF : lo % HALF + hi - lo]

        def project(t):
            for lo, hi in HALVES if t == 0 else WHOLE:
                bank = PACK if (t, lo) == (0, 0) else t
                acc = product(bank, w_codes, w_scales, t, xq_codes, xq_scales, lo, hi)
                leave_psum(acc, y_win[t], y_plain[t], lo, hi, gain[:, t : t + 1], gain[:, t : t + 1])

        def first_difference(t):
            for lo, hi in HALVES if t in (0, LAST) else WHOLE:
                gather_with(neg_st_at(t, lo, hi), y_win[t], n1_l, y_plain[t][:, lo:hi], ALU.subtract, lo, hi)
            for lo, hi in HALVES if t == LAST else WHOLE:
                nc.scalar.activation(neg_half_st[t][:, lo:hi], neg_st_at(t, lo, hi), COPY, scale=0.5)

        project(0)
        for t in range(1, PACK):
            project(t)
            first_difference(t - 1)
        first_difference(LAST)

        z_codes = keep.tile([P, S], U32, name="z_codes", align_bytes=64)
        z_scales = keep.tile([P, S], U8, name="z_scales", align_bytes=64)
        s_win, neg_s = twin_tiles("s", (1, 2, 3))
        z_sizes = [PACK * (hi - lo) for lo, hi in Z_RANGES]
        overlap_at = z_sizes[2] // PACK * LAST
        reused = keep.tile([P, overlap_at + z_sizes[0] // 2], F32, name="reused", tag="neg_st_last0", align_bytes=64)
        z_f32 = [
            keep.tile([P, z_sizes[0]], F32, name="z_f32_0")[:],
            keep.tile([P, z_sizes[1]], F32, name="z_f32_1")[:],
            reused[:, 0 : z_sizes[2]],
        ]
        z_bf = [
            reused[:, overlap_at : overlap_at + z_sizes[0] // 2].bitcast(BF16),
            keep.tile([P, z_sizes[1]], BF16, name="z_bf_1", align_bytes=64)[:],
            keep.tile([P, z_sizes[2]], BF16, name="z_bf_2", align_bytes=64)[:],
        ]

        def z_gather(r, t):
            lo, hi = Z_RANGES[r]
            dst = z_f32[r][:, t * (hi - lo) : (t + 1) * (hi - lo)]
            gather_with(dst, neg_half_st[t], n1_l, neg_st_at(t, lo, hi), ALU.subtract, lo, hi)

        def z_round(r, copy):
            copy(
                z_bf[r].rearrange("p (c i t) -> p c t i", i=LINE, t=PACK),
                z_f32[r].rearrange("p (t c i) -> p c t i", i=LINE, t=PACK),
            )

        def z_quantize(r):
            lo, hi = Z_RANGES[r]
            nc.vector.quantize_mx(out=z_codes[:, lo:hi].bitcast(FP8X4), scales=z_scales[:, lo:hi], in_=z_bf[r])

        def scores(bank, t, lo, hi):
            acc = product(bank, cand_codes, cand_scales, t, z_codes, z_scales, lo, hi)
            leave_psum(acc, s_win[t], neg_s[t], lo, hi, SCORE_SCALE, -SCORE_SCALE)

        for t in range(PACK):
            z_gather(0, t)
            z_gather(1, t)
        z_round(0, nc.scalar.copy)
        z_round(1, nc.scalar.copy)
        for t in range(LAST):
            z_gather(2, t)
        z_quantize(0)
        scores(5, 0, *Z_RANGES[0])
        z_gather(2, LAST)
        z_quantize(1)
        scores(6, 0, *Z_RANGES[1])
        z_round(2, nc.vector.tensor_copy)
        z_quantize(2)
        scores(7, 0, *Z_RANGES[2])
        scores(1, 1, 0, S)

        out_rows = out.rearrange("(p t) n -> p t n", t=PACK)
        da = [keep.tile([P, S], F32, name=f"da{t}") for t in range(PACK)]
        db = [keep.tile([P, S], F32, name=f"db{t}") for t in range(PACK)]
        upper = [keep.tile([P, S], F32, name=f"upper{t}") for t in range(PACK)]
        res = [keep.tile([P, S], F32, name=f"res{t}") for t in range(PACK)]
        identity = keep.tile([P, P], F32, name="identity")
        make_identity(nc, identity[:])

        def fetch(dst, lst, t, lo=0, hi=S):
            gather_with(dst[t][:, lo:hi], s_win[t], lst, neg_s[t][:, lo:hi], ALU.add, lo, hi)

        def clip_above(t, lo=0, hi=S):
            nc.vector.scalar_tensor_tensor(upper[t][:, lo:hi], da[t][:, lo:hi], 0.0, db[t][:, lo:hi], ALU.max, ALU.min)

        def clip_below(step, t, lo, hi):
            nc.vector.scalar_tensor_tensor(step[:, lo:hi], da[t][:, lo:hi], 0.0, upper[t][:, lo:hi], ALU.min, ALU.max)

        def turned_sum(dst, bank, terms, func=COPY, scale=1.0):
            total = psum.tile([P, S], F32, name=f"total{bank}", tag=f"bank{bank}")
            for at in range(0, S, P):
                for n, term in enumerate(terms):
                    nc.tensor.matmul(
                        total[:, at : at + P],
                        term[:, at : at + P],
                        identity[:],
                        start=n == 0,
                        stop=n == len(terms) - 1,
                        is_transpose=True,
                    )
            nc.scalar.activation(dst[:], total[:], func, scale=scale)

        def lower_end(t):
            drop = keep.tile([P, S], F32, name=f"drop{t}")
            nc.scalar.activation(drop[:], da[t][:], RELU, scale=-1.0)
            low = keep.tile([P, S], F32, name=f"low{t}")
            turned_sum(low, 4, (neg_s[t], drop), scale=-1.0)
            return drop, low

        def finish_on_tensor(t, drop, low):
            rise = keep.tile([P, S], F32, name=f"rise{t}")
            turned_sum(rise, 5, (drop, upper[t]), RELU)
            turned_sum(res[t], 6, (low, rise))
            nc.scalar.dma_start(out_rows[:, t, :], res[t][:])

        def finish_on_vector(step, t, lo, hi):
            nc.vector.tensor_tensor(res[t][:, lo:hi], step[:, lo:hi], neg_s[t][:, lo:hi], ALU.subtract)
            nc.sync.dma_start(out_rows[:, t, lo:hi], res[t][:, lo:hi])

        by_halves(fetch, da, n2_l, 0)
        ends0 = lower_end(0)
        scores(2, 2, 0, S)
        by_halves(fetch, db, n3_l, 0)
        fetch(da, n2_l, 1)
        clip_above(0)
        finish_on_tensor(0, *ends0)
        ends1 = lower_end(1)
        scores(3, 3, 0, S)
        fetch(db, n3_l, 1)
        fetch(da, n2_l, 2)
        clip_above(1)
        finish_on_tensor(1, *ends1)
        for t in (2, LAST):
            by_halves(fetch, db, n3_l, t)
            by_halves(clip_above, t)
            step = keep.tile([P, S], F32, name=f"step{t}")
            by_halves(clip_below, step, t)
            by_halves(finish_on_vector, step, t)
            if t < LAST:
                fetch(da, n2_l, t + 1)
